import numpy as np
import ml_dtypes


def mxq(x, axis, fmt="e4m3"):
    dtype, down = {"e4m3": (ml_dtypes.float8_e4m3fn, 7), "e5m2": (ml_dtypes.float8_e5m2, 14)}[fmt]
    v = np.moveaxis(np.asarray(x, np.float32).astype(ml_dtypes.bfloat16).astype(np.float64), axis, -1)
    blocks = v.reshape(v.shape[:-1] + (-1, 32))
    amax = np.abs(blocks).max(-1, keepdims=True)
    byte = np.maximum(np.where(amax > 0, np.frexp(amax)[1] - 1 + 127, 0) - down, 1)
    scale = np.exp2(byte - 127.0)
    codes = (blocks / scale).astype(np.float32).astype(dtype).astype(np.float64)
    return np.moveaxis((codes * scale).reshape(v.shape), -1, axis)


WIDE = False


def mx_kscale(k):
    if not WIDE:
        return np.ones(k)
    levels = np.array([10, -10, 5, -5, 0])
    if k % 512:
        return np.exp2(np.random.permutation(np.resize(levels, k // 32))).repeat(32)
    a = np.empty((k // 512, 16))
    for p in range(k // 512):
        a[p, :8] = np.random.permutation(np.resize(levels, 8))
        for g in range(8):
            far = levels[np.abs(levels - a[p, g]) >= 10]
            a[p, g + 8] = far[np.random.randint(len(far))]
    return np.exp2(a.ravel()).repeat(32)


def f64(x):
    return np.asarray(x).astype(np.float64)


def striped(idx):
    return np.tile(idx.reshape(-1, 16).T, (8, 1)).astype(np.uint16)


def unstriped(offs):
    return offs[:16].T.reshape(-1).astype(np.int64)


def pack_weight(w):
    k, n = w.shape
    w = f64(np.asarray(w, np.float32).astype(ml_dtypes.bfloat16)).reshape(k // 32, 32, n)
    amax = np.abs(w).max(1)
    byte = np.clip(np.where(amax > 0, np.frexp(amax)[1] - 1 + 127 - 7, 1), 1, 254)
    scaled = (w * np.exp2(127.0 - byte)[:, None, :]).reshape(k, n).astype(np.float32)
    words = np.ascontiguousarray(scaled.reshape(k // 512, 128, 4, n).transpose(0, 1, 3, 2)).astype(ml_dtypes.float8_e4m3fn).view(np.uint8)
    return words, np.ascontiguousarray(byte.astype(np.uint8).reshape(k // 512, 16, n))


def unpack_weight(words, scales):
    g, p, n, _ = words.shape
    vals = np.ascontiguousarray(words).view(ml_dtypes.float8_e4m3fn).astype(np.float64) * np.repeat(np.exp2(scales.astype(np.float64) - 127.0), 8, axis=1)[..., None]
    return vals.transpose(0, 1, 3, 2).reshape(g * 512, n)


def relu(v):
    return np.maximum(v, 0.0)


def sigmoid(v):
    return 1.0 / (1.0 + np.exp(-np.maximum(v, -700.0)))


K, T, N, U = 512, 512, 256, 1024


def setup_inputs():
    n = np.random.standard_normal
    s = mx_kscale(K)[:, None]
    packed_xT = pack_weight(n((K, T)) * s)
    return {
        "x_words": packed_xT[0],
        "x_scales": packed_xT[1],
        "mem": n((N, U)).astype(np.float32),
        "w1": (n((K, N)) / np.sqrt(K) / s).astype(np.float32),
        "w2": (n((K, N)) / np.sqrt(K) / s).astype(np.float32),
        "slot": striped(np.random.permutation(U)[:T]),
    }


def reference(x_words, x_scales, mem, w1, w2, slot):
    old = f64(mem)[:, unstriped(slot)]
    xq = unpack_weight(x_words, x_scales)
    g = sigmoid(mxq(f64(w2), 0, "e4m3").T @ xq)
    y = relu(mxq(f64(w1), 0, "e4m3").T @ xq)
    out = f64(mem).copy()
    out[:, unstriped(slot)] = old + g * (y - old)
    return out

@@ -1,0 +1,114 @@
+from contextlib import ExitStack
+
+import concourse.mybir as mybir
+
+F32 = mybir.dt.float32
+BF16 = mybir.dt.bfloat16
+I32 = mybir.dt.int32
+U32 = mybir.dt.uint32
+U16 = mybir.dt.uint16
+U8 = mybir.dt.uint8
+FP8X4 = mybir.dt.float8_e4m3fn_x4
+ALU = mybir.AluOpType
+ACT = mybir.ActivationFunctionType
+
+P = 128
+PACK = 4
+K, T, N, U = 512, 512, 256, 1024
+FLOPS = 2 * 2 * K * N * T
+
+
+def tile_picked_wgmem_relu_l_kernel(tc, x_words, x_scales, mem, w1, w2, slot, out):
+    nc = tc.nc
+    with ExitStack() as ctx:
+        keep = ctx.enter_context(tc.tile_pool(name="keep", bufs=1))
+        psum = ctx.enter_context(tc.psum_pool(name="psum", bufs=1))
+
+        offsets = keep.tile([P, T // 16], U16, name="offsets")
+        x_codes = keep.tile([P, T], U32, name="x_codes", align_bytes=64)
+        x_plane = keep.tile([P, T], U8, name="x_plane", align_bytes=64)
+        windows = [keep.tile([P, U], F32, name="window%d" % b) for b in range(2)]
+        raw = {}
+        for b in range(2):
+            for name in ("gate", "cand"):
+                raw[name, b] = keep.tile([P, PACK, P], F32, name="raw_%s%d" % (name, b))
+
+        def load_weights(name, w, b):
+            nc.sync.dma_start(out=raw[name, b][:], in_=w[:, b * P : (b + 1) * P].rearrange("(p j) m -> p j m", j=PACK))
+
+        nc.vector.memset(x_plane[:].bitcast(I32), 0)
+        load_weights("gate", w2, 0)
+        nc.sync.dma_start(out=x_codes[:].bitcast(I32), in_=x_words[0].rearrange("p n t -> p (n t)").bitcast(I32))
+        for q in range(4):
+            queue = nc.sync if q % 2 == 0 else nc.scalar
+            queue.dma_start(
+                out=x_plane[32 * q : 32 * q + 4, :].bitcast(I32),
+                in_=x_scales[0, 4 * q : 4 * q + 4, :].bitcast(I32),
+            )
+        load_weights("cand", w1, 0)
+        load_weights("gate", w2, 1)
+        load_weights("cand", w1, 1)
+        nc.sync.dma_start(out=windows[0][:], in_=mem[0:P, :])
+        nc.sync.dma_start(offsets[:], slot)
+        nc.sync.dma_start(out=windows[1][:], in_=mem[P : 2 * P, :])
+
+        codes = {}
+        planes = {}
+
+        def quantise(name, b):
+            grouped = keep.tile([P, P, PACK], BF16, name="grouped_%s%d" % (name, b), align_bytes=64)
+            src = raw[name, b][:].rearrange("p j (c i) -> p c j i", i=4)
+            dst = grouped[:].rearrange("p (c i) j -> p c j i", i=4)
+            nc.vector.tensor_copy(out=dst, in_=src)
+            codes[name, b] = keep.tile([P, P], U32, name="codes_%s%d" % (name, b), align_bytes=64)
+            planes[name, b] = keep.tile([P, P], U8, name="plane_%s%d" % (name, b), align_bytes=64)
+            nc.vector.quantize_mx(
+                out=codes[name, b][:].bitcast(FP8X4),
+                scales=planes[name, b][:],
+                in_=grouped[:].rearrange("p m j -> p (m j)"),
+            )
+
+        def product(name, b, cols):
+            width = cols.stop - cols.start
+            acc = psum.tile([P, width], F32, name="acc_%s%d_%d" % (name, b, cols.start))
+            nc.tensor.matmul_mx(
+                out=acc[:],
+                lhsT=codes[name, b][:].bitcast(FP8X4),
+                lhsT_scale=planes[name, b][:],
+                rhs=x_codes[:, cols].bitcast(FP8X4),
+                rhs_scale=x_plane[:, cols],
+                start=True,
+                stop=True,
+            )
+            return acc
+
+        def blend(b, cols, kept, fresh):
+            width = cols.stop - cols.start
+            gate_sum = product("gate", b, cols)
+            cand_sum = product("cand", b, cols)
+            gate = keep.tile([P, width], F32, name="gate%d_%d" % (b, cols.start))
+            rest = keep.tile([P, width], F32, name="rest%d_%d" % (b, cols.start))
+            nc.scalar.activation(out=gate[:], in_=gate_sum[:], func=ACT.Sigmoid)
+            nc.scalar.activation(out=rest[:], in_=gate_sum[:], func=ACT.Sigmoid, scale=-1.0)
+            nc.vector.scalar_tensor_tensor(
+                out=fresh[:, cols], in0=cand_sum[:], scalar=0.0, in1=gate[:], op0=ALU.max, op1=ALU.mult
+            )
+            nc.vector.tensor_tensor(
+                out=kept[:, cols],
+                in0=windows[b][:].indirect(offsets[:, cols.start // 16 : cols.stop // 16]),
+                in1=rest[:],
+                op=ALU.mult,
+            )
+
+        for b in range(2):
+            quantise("gate", b)
+            quantise("cand", b)
+        kept = [keep.tile([P, T], F32, name="kept%d" % b) for b in range(2)]
+        fresh = [keep.tile([P, T], F32, name="fresh%d" % b) for b in range(2)]
+        for b in range(2):
+            blend(b, slice(0, T), kept[b], fresh[b])
+        for b in range(2):
+            nc.vector.tensor_tensor(
+                out=windows[b][:].indirect(offsets[:]), in0=kept[b][:], in1=fresh[b][:], op=ALU.add
+            )
+            nc.sync.dma_start(out=out[b * P : (b + 1) * P, :], in_=windows[b][:])

@@ -38,14 +38,13 @@ def tile_picked_wgmem_relu_l_kernel(tc, x_words, x_scales, mem, w1, w2, slot, ou
 
         nc.vector.memset(x_plane[:].bitcast(I32), 0)
         load_weights("gate", w2, 0)
-        nc.sync.dma_start(out=x_codes[:].bitcast(I32), in_=x_words[0].rearrange("p n t -> p (n t)").bitcast(I32))
+        load_weights("cand", w1, 0)
         for q in range(4):
-            queue = nc.sync if q % 2 == 0 else nc.scalar
-            queue.dma_start(
+            nc.sync.dma_start(
                 out=x_plane[32 * q : 32 * q + 4, :].bitcast(I32),
                 in_=x_scales[0, 4 * q : 4 * q + 4, :].bitcast(I32),
             )
-        load_weights("cand", w1, 0)
+        nc.sync.dma_start(out=x_codes[:].bitcast(I32), in_=x_words[0].rearrange("p n t -> p (n t)").bitcast(I32))
         load_weights("gate", w2, 1)
         load_weights("cand", w1, 1)
         nc.sync.dma_start(out=windows[0][:], in_=mem[0:P, :])
@@ -82,33 +81,38 @@ def tile_picked_wgmem_relu_l_kernel(tc, x_words, x_scales, mem, w1, w2, slot, ou
             )
             return acc
 
-        def blend(b, cols, kept, fresh):
-            width = cols.stop - cols.start
-            gate_sum = product("gate", b, cols)
-            cand_sum = product("cand", b, cols)
-            gate = keep.tile([P, width], F32, name="gate%d_%d" % (b, cols.start))
-            rest = keep.tile([P, width], F32, name="rest%d_%d" % (b, cols.start))
-            nc.scalar.activation(out=gate[:], in_=gate_sum[:], func=ACT.Sigmoid)
-            nc.scalar.activation(out=rest[:], in_=gate_sum[:], func=ACT.Sigmoid, scale=-1.0)
-            nc.vector.scalar_tensor_tensor(
-                out=fresh[:, cols], in0=cand_sum[:], scalar=0.0, in1=gate[:], op0=ALU.max, op1=ALU.mult
-            )
-            nc.vector.tensor_tensor(
-                out=kept[:, cols],
-                in0=windows[b][:].indirect(offsets[:, cols.start // 16 : cols.stop // 16]),
-                in1=rest[:],
-                op=ALU.mult,
-            )
-
+        every = slice(0, T)
         for b in range(2):
             quantise("gate", b)
             quantise("cand", b)
+        sums = {(name, b): product(name, b, every) for b in range(2) for name in ("gate", "cand")}
+        gate = [keep.tile([P, T], F32, name="gate%d" % b) for b in range(2)]
+        rest = [keep.tile([P, T], F32, name="rest%d" % b) for b in range(2)]
         kept = [keep.tile([P, T], F32, name="kept%d" % b) for b in range(2)]
-        fresh = [keep.tile([P, T], F32, name="fresh%d" % b) for b in range(2)]
         for b in range(2):
-            blend(b, slice(0, T), kept[b], fresh[b])
-        for b in range(2):
-            nc.vector.tensor_tensor(
-                out=windows[b][:].indirect(offsets[:]), in0=kept[b][:], in1=fresh[b][:], op=ALU.add
+            nc.scalar.activation(out=gate[b][:], in_=sums["gate", b][:], func=ACT.Sigmoid)
+            nc.scalar.activation(out=rest[b][:], in_=sums["gate", b][:], func=ACT.Sigmoid, scale=-1.0)
+        cand1 = keep.tile([P, T], F32, name="cand1")
+        nc.scalar.activation(out=cand1[:], in_=sums["cand", 1][:], func=ACT.Relu)
+
+        fresh0 = keep.tile([P, T], F32, name="fresh0", tag="fresh")
+        nc.vector.scalar_tensor_tensor(
+            out=fresh0[:], in0=sums["cand", 0][:], scalar=0.0, in1=gate[0][:], op0=ALU.max, op1=ALU.mult
+        )
+        nc.vector.tensor_tensor(out=kept[0][:], in0=windows[0][:].indirect(offsets[:]), in1=rest[0][:], op=ALU.mult)
+        new0 = keep.tile([P, T], F32, name="new0")
+        halves = [slice(0, T // 2), slice(T // 2, T)]
+        for cols in halves:
+            nc.gpsimd.tensor_tensor(out=new0[:, cols], in0=kept[0][:, cols], in1=fresh0[:, cols], op=ALU.add)
+        old1 = keep.tile([P, T], F32, name="old1")
+        nc.vector.tensor_copy(out=old1[:], in_=windows[1][:].indirect(offsets[:]))
+        for cols in halves:
+            nc.vector.tensor_copy(
+                out=windows[0][:].indirect(offsets[:, cols.start // 16 : cols.stop // 16]), in_=new0[:, cols]
             )
-            nc.sync.dma_start(out=out[b * P : (b + 1) * P, :], in_=windows[b][:])
+        nc.sync.dma_start(out=out[0:P, :], in_=windows[0][:])
+        fresh1 = keep.tile([P, T], F32, name="fresh1", tag="fresh")
+        nc.gpsimd.tensor_tensor(out=fresh1[:], in0=cand1[:], in1=gate[1][:], op=ALU.mult)
+        nc.gpsimd.tensor_tensor(out=kept[1][:], in0=old1[:], in1=rest[1][:], op=ALU.mult)
+        nc.vector.tensor_tensor(out=windows[1][:].indirect(offsets[:]), in0=kept[1][:], in1=fresh1[:], op=ALU.add)
+        nc.sync.dma_start(out=out[P : 2 * P, :], in_=windows[1][:])

@@ -92,8 +92,8 @@ def tile_picked_wgmem_relu_l_kernel(tc, x_words, x_scales, mem, w1, w2, slot, ou
         for b in range(2):
             nc.scalar.activation(out=gate[b][:], in_=sums["gate", b][:], func=ACT.Sigmoid)
             nc.scalar.activation(out=rest[b][:], in_=sums["gate", b][:], func=ACT.Sigmoid, scale=-1.0)
-        cand1 = keep.tile([P, T], F32, name="cand1")
-        nc.scalar.activation(out=cand1[:], in_=sums["cand", 1][:], func=ACT.Relu)
+        cand1 = keep.tile([P, T // 2], F32, name="cand1")
+        nc.scalar.activation(out=cand1[:], in_=sums["cand", 1][:, T // 2 :], func=ACT.Relu)
 
         fresh0 = keep.tile([P, T], F32, name="fresh0", tag="fresh")
         nc.vector.scalar_tensor_tensor(
@@ -106,13 +106,15 @@ def tile_picked_wgmem_relu_l_kernel(tc, x_words, x_scales, mem, w1, w2, slot, ou
             nc.gpsimd.tensor_tensor(out=new0[:, cols], in0=kept[0][:, cols], in1=fresh0[:, cols], op=ALU.add)
         old1 = keep.tile([P, T], F32, name="old1")
         nc.vector.tensor_copy(out=old1[:], in_=windows[1][:].indirect(offsets[:]))
-        for cols in halves:
-            nc.vector.tensor_copy(
-                out=windows[0][:].indirect(offsets[:, cols.start // 16 : cols.stop // 16]), in_=new0[:, cols]
-            )
-        nc.sync.dma_start(out=out[0:P, :], in_=windows[0][:])
+        first, second = halves
+        nc.vector.tensor_copy(out=windows[0][:].indirect(offsets[:, : T // 32]), in_=new0[:, first])
         fresh1 = keep.tile([P, T], F32, name="fresh1", tag="fresh")
-        nc.gpsimd.tensor_tensor(out=fresh1[:], in0=cand1[:], in1=gate[1][:], op=ALU.mult)
+        nc.vector.scalar_tensor_tensor(
+            out=fresh1[:, first], in0=sums["cand", 1][:, first], scalar=0.0, in1=gate[1][:, first], op0=ALU.max, op1=ALU.mult
+        )
+        nc.vector.tensor_copy(out=windows[0][:].indirect(offsets[:, T // 32 :]), in_=new0[:, second])
+        nc.sync.dma_start(out=out[0:P, :], in_=windows[0][:])
+        nc.gpsimd.tensor_tensor(out=fresh1[:, second], in0=cand1[:], in1=gate[1][:, second], op=ALU.mult)
         nc.gpsimd.tensor_tensor(out=kept[1][:], in0=old1[:], in1=rest[1][:], op=ALU.mult)
         nc.vector.tensor_tensor(out=windows[1][:].indirect(offsets[:]), in0=kept[1][:], in1=fresh1[:], op=ALU.add)
         nc.sync.dma_start(out=out[P : 2 * P, :], in_=windows[1][:])

@@ -31,7 +31,7 @@ def tile_picked_wgmem_relu_l_kernel(tc, x_words, x_scales, mem, w1, w2, slot, ou
         raw = {}
         for b in range(2):
             for name in ("gate", "cand"):
-                raw[name, b] = keep.tile([P, PACK, P], F32, name="raw_%s%d" % (name, b))
+                raw[name, b] = keep.tile([P, PACK, P], F32, name="raw_%s%d" % (name, b), tag="raw_%s%d" % (name, b))
 
         def load_weights(name, w, b):
             nc.sync.dma_start(out=raw[name, b][:], in_=w[:, b * P : (b + 1) * P].rearrange("(p j) m -> p j m", j=PACK))
@@ -46,25 +46,31 @@ def tile_picked_wgmem_relu_l_kernel(tc, x_words, x_scales, mem, w1, w2, slot, ou
             )
         nc.sync.dma_start(out=x_codes[:].bitcast(I32), in_=x_words[0].rearrange("p n t -> p (n t)").bitcast(I32))
         load_weights("gate", w2, 1)
-        load_weights("cand", w1, 1)
         nc.sync.dma_start(out=windows[0][:], in_=mem[0:P, :])
         nc.sync.dma_start(offsets[:], slot)
+        load_weights("cand", w1, 1)
         nc.sync.dma_start(out=windows[1][:], in_=mem[P : 2 * P, :])
 
         codes = {}
         planes = {}
+        grouped = {}
+
+        def cast(name, b, on_scalar):
+            grouped[name, b] = keep.tile([P, P, PACK], BF16, name="grouped_%s%d" % (name, b), tag="grouped_%s%d" % (name, b), align_bytes=64)
+            src = raw[name, b][:].rearrange("p j (c i) -> p c j i", i=4)
+            dst = grouped[name, b][:].rearrange("p (c i) j -> p c j i", i=4)
+            if on_scalar:
+                nc.scalar.copy(out=dst, in_=src)
+            else:
+                nc.vector.tensor_copy(out=dst, in_=src)
 
         def quantise(name, b):
-            grouped = keep.tile([P, P, PACK], BF16, name="grouped_%s%d" % (name, b), align_bytes=64)
-            src = raw[name, b][:].rearrange("p j (c i) -> p c j i", i=4)
-            dst = grouped[:].rearrange("p (c i) j -> p c j i", i=4)
-            nc.vector.tensor_copy(out=dst, in_=src)
             codes[name, b] = keep.tile([P, P], U32, name="codes_%s%d" % (name, b), align_bytes=64)
             planes[name, b] = keep.tile([P, P], U8, name="plane_%s%d" % (name, b), align_bytes=64)
             nc.vector.quantize_mx(
                 out=codes[name, b][:].bitcast(FP8X4),
                 scales=planes[name, b][:],
-                in_=grouped[:].rearrange("p m j -> p (m j)"),
+                in_=grouped[name, b][:].rearrange("p m j -> p (m j)"),
             )
 
         def product(name, b, cols):
@@ -81,40 +87,59 @@ def tile_picked_wgmem_relu_l_kernel(tc, x_words, x_scales, mem, w1, w2, slot, ou
             )
             return acc
 
-        every = slice(0, T)
-        for b in range(2):
-            quantise("gate", b)
-            quantise("cand", b)
-        sums = {(name, b): product(name, b, every) for b in range(2) for name in ("gate", "cand")}
-        gate = [keep.tile([P, T], F32, name="gate%d" % b) for b in range(2)]
-        rest = [keep.tile([P, T], F32, name="rest%d" % b) for b in range(2)]
-        kept = [keep.tile([P, T], F32, name="kept%d" % b) for b in range(2)]
-        for b in range(2):
-            nc.scalar.activation(out=gate[b][:], in_=sums["gate", b][:], func=ACT.Sigmoid)
-            nc.scalar.activation(out=rest[b][:], in_=sums["gate", b][:], func=ACT.Sigmoid, scale=-1.0)
-        cand1 = keep.tile([P, T // 2], F32, name="cand1")
-        nc.scalar.activation(out=cand1[:], in_=sums["cand", 1][:, T // 2 :], func=ACT.Relu)
+        def entries(cols):
+            return offsets[:, cols.start // 16 : cols.stop // 16]
 
-        fresh0 = keep.tile([P, T], F32, name="fresh0", tag="fresh")
-        nc.vector.scalar_tensor_tensor(
-            out=fresh0[:], in0=sums["cand", 0][:], scalar=0.0, in1=gate[0][:], op0=ALU.max, op1=ALU.mult
-        )
-        nc.vector.tensor_tensor(out=kept[0][:], in0=windows[0][:].indirect(offsets[:]), in1=rest[0][:], op=ALU.mult)
-        new0 = keep.tile([P, T], F32, name="new0")
+        def wide(name):
+            return keep.tile([P, T], F32, name=name, tag=name)
+
+        every = slice(0, T)
+
+        for name, b in (("gate", 0), ("cand", 0), ("gate", 1)):
+            cast(name, b, False)
+            quantise(name, b)
         halves = [slice(0, T // 2), slice(T // 2, T)]
-        for cols in halves:
-            nc.gpsimd.tensor_tensor(out=new0[:, cols], in0=kept[0][:, cols], in1=fresh0[:, cols], op=ALU.add)
-        old1 = keep.tile([P, T], F32, name="old1")
-        nc.vector.tensor_copy(out=old1[:], in_=windows[1][:].indirect(offsets[:]))
         first, second = halves
-        nc.vector.tensor_copy(out=windows[0][:].indirect(offsets[:, : T // 32]), in_=new0[:, first])
-        fresh1 = keep.tile([P, T], F32, name="fresh1", tag="fresh")
+        kept0, fresh0, old1 = wide("kept0"), wide("fresh0"), wide("old1")
+        rest0, gate0 = wide("rest0"), wide("gate0")
+        u0 = {cols.start: product("gate", 0, cols) for cols in halves}
+        v0 = {cols.start: product("cand", 0, cols) for cols in halves}
+        for cols in halves:
+            nc.scalar.activation(out=gate0[:, cols], in_=u0[cols.start][:], func=ACT.Sigmoid)
+        for cols in halves:
+            nc.scalar.activation(out=rest0[:, cols], in_=u0[cols.start][:], func=ACT.Sigmoid, scale=-1.0)
+        for cols in halves:
+            nc.vector.scalar_tensor_tensor(
+                out=fresh0[:, cols], in0=v0[cols.start][:], scalar=0.0, in1=gate0[:, cols], op0=ALU.max, op1=ALU.mult
+            )
+        for cols in halves:
+            nc.vector.tensor_tensor(
+                out=kept0[:, cols], in0=windows[0][:].indirect(entries(cols)), in1=rest0[:, cols], op=ALU.mult
+            )
+        u1 = product("gate", 1, every)
+        cast("cand", 1, True)
+        quantise("cand", 1)
+        nc.vector.tensor_copy(out=old1[:], in_=windows[1][:].indirect(offsets[:]))
+        new0 = keep.tile([P, T], F32, name="new0", tag="grouped_cand1", align_bytes=64)
+        lead, tail = slice(0, T // 4), slice(T // 4, T)
+        for cols in (lead, tail):
+            nc.gpsimd.tensor_tensor(out=new0[:, cols], in0=kept0[:, cols], in1=fresh0[:, cols], op=ALU.add)
+        v1 = {cols.start: product("cand", 1, cols) for cols in halves}
+        kept1 = wide("kept1")
+        sigmoids1 = keep.tile([P, 2 * T], F32, name="sigmoids1", tag="raw_cand1")
+        gate1, rest1 = sigmoids1[:, :T], sigmoids1[:, T:]
+        cand1 = keep.tile([P, T // 2], F32, name="cand1")
+        nc.scalar.activation(out=gate1, in_=u1[:], func=ACT.Sigmoid)
+        nc.scalar.activation(out=rest1, in_=u1[:], func=ACT.Sigmoid, scale=-1.0)
+        nc.scalar.activation(out=cand1[:], in_=v1[T // 2][:], func=ACT.Relu)
+        nc.vector.tensor_copy(out=windows[0][:].indirect(entries(lead)), in_=new0[:, lead])
+        fresh1 = keep.tile([P, T], F32, name="fresh1", tag="fresh0")
         nc.vector.scalar_tensor_tensor(
-            out=fresh1[:, first], in0=sums["cand", 1][:, first], scalar=0.0, in1=gate[1][:, first], op0=ALU.max, op1=ALU.mult
+            out=fresh1[:, first], in0=v1[0][:], scalar=0.0, in1=gate1[:, first], op0=ALU.max, op1=ALU.mult
         )
-        nc.vector.tensor_copy(out=windows[0][:].indirect(offsets[:, T // 32 :]), in_=new0[:, second])
+        nc.vector.tensor_copy(out=windows[0][:].indirect(entries(tail)), in_=new0[:, tail])
         nc.sync.dma_start(out=out[0:P, :], in_=windows[0][:])
-        nc.gpsimd.tensor_tensor(out=fresh1[:, second], in0=cand1[:], in1=gate[1][:, second], op=ALU.mult)
-        nc.gpsimd.tensor_tensor(out=kept[1][:], in0=old1[:], in1=rest[1][:], op=ALU.mult)
-        nc.vector.tensor_tensor(out=windows[1][:].indirect(offsets[:]), in0=kept[1][:], in1=fresh1[:], op=ALU.add)
+        nc.gpsimd.tensor_tensor(out=fresh1[:, second], in0=cand1[:], in1=gate1[:, second], op=ALU.mult)
+        nc.gpsimd.tensor_tensor(out=kept1[:], in0=old1[:], in1=rest1, op=ALU.mult)
+        nc.vector.tensor_tensor(out=windows[1][:].indirect(offsets[:]), in0=kept1[:], in1=fresh1[:], op=ALU.add)
         nc.sync.dma_start(out=out[P : 2 * P, :], in_=windows[1][:])

@@ -100,7 +100,10 @@ def tile_picked_wgmem_relu_l_kernel(tc, x_words, x_scales, mem, w1, w2, slot, ou
             quantise(name, b)
         halves = [slice(0, T // 2), slice(T // 2, T)]
         first, second = halves
-        kept0, fresh0, old1 = wide("kept0"), wide("fresh0"), wide("old1")
+        kept0, fresh0 = wide("kept0"), wide("fresh0")
+        lead, tail = slice(0, T // 4), slice(T // 4, T)
+        fresh0_lead = keep.tile([P, T // 4], F32, name="fresh0_lead", tag="lead")
+        old1 = keep.tile([P, T - T // 4], F32, name="old1")
         rest0, gate0 = wide("rest0"), wide("gate0")
         u0 = {cols.start: product("gate", 0, cols) for cols in halves}
         v0 = {cols.start: product("cand", 0, cols) for cols in halves}
@@ -108,10 +111,12 @@ def tile_picked_wgmem_relu_l_kernel(tc, x_words, x_scales, mem, w1, w2, slot, ou
             nc.scalar.activation(out=gate0[:, cols], in_=u0[cols.start][:], func=ACT.Sigmoid)
         for cols in halves:
             nc.scalar.activation(out=rest0[:, cols], in_=u0[cols.start][:], func=ACT.Sigmoid, scale=-1.0)
-        for cols in halves:
-            nc.vector.scalar_tensor_tensor(
-                out=fresh0[:, cols], in0=v0[cols.start][:], scalar=0.0, in1=gate0[:, cols], op0=ALU.max, op1=ALU.mult
-            )
+        for cols, bank, target in (
+            (lead, v0[0][:, lead], fresh0_lead[:]),
+            (slice(T // 4, T // 2), v0[0][:, T // 4 :], fresh0[:, T // 4 : T // 2]),
+            (second, v0[T // 2][:], fresh0[:, second]),
+        ):
+            nc.vector.scalar_tensor_tensor(out=target, in0=bank, scalar=0.0, in1=gate0[:, cols], op0=ALU.max, op1=ALU.mult)
         for cols in halves:
             nc.vector.tensor_tensor(
                 out=kept0[:, cols], in0=windows[0][:].indirect(entries(cols)), in1=rest0[:, cols], op=ALU.mult
@@ -119,27 +124,25 @@ def tile_picked_wgmem_relu_l_kernel(tc, x_words, x_scales, mem, w1, w2, slot, ou
         u1 = product("gate", 1, every)
         cast("cand", 1, True)
         quantise("cand", 1)
-        nc.vector.tensor_copy(out=old1[:], in_=windows[1][:].indirect(offsets[:]))
+        nc.vector.tensor_copy(out=old1[:], in_=windows[1][:].indirect(entries(tail)))
         new0 = keep.tile([P, T], F32, name="new0", tag="grouped_cand1", align_bytes=64)
-        lead, tail = slice(0, T // 4), slice(T // 4, T)
-        for cols in (lead, tail):
-            nc.gpsimd.tensor_tensor(out=new0[:, cols], in0=kept0[:, cols], in1=fresh0[:, cols], op=ALU.add)
-        v1 = {cols.start: product("cand", 1, cols) for cols in halves}
+        nc.gpsimd.tensor_tensor(out=new0[:, lead], in0=kept0[:, lead], in1=fresh0_lead[:], op=ALU.add)
+        nc.gpsimd.tensor_tensor(out=new0[:, tail], in0=kept0[:, tail], in1=fresh0[:, tail], op=ALU.add)
+        v1 = product("cand", 1, every)
         kept1 = wide("kept1")
         sigmoids1 = keep.tile([P, 2 * T], F32, name="sigmoids1", tag="raw_cand1")
         gate1, rest1 = sigmoids1[:, :T], sigmoids1[:, T:]
-        cand1 = keep.tile([P, T // 2], F32, name="cand1")
+        cand1, fresh1 = wide("cand1"), wide("fresh1")
         nc.scalar.activation(out=gate1, in_=u1[:], func=ACT.Sigmoid)
         nc.scalar.activation(out=rest1, in_=u1[:], func=ACT.Sigmoid, scale=-1.0)
-        nc.scalar.activation(out=cand1[:], in_=v1[T // 2][:], func=ACT.Relu)
+        nc.scalar.activation(out=cand1[:], in_=v1[:], func=ACT.Relu)
         nc.vector.tensor_copy(out=windows[0][:].indirect(entries(lead)), in_=new0[:, lead])
-        fresh1 = keep.tile([P, T], F32, name="fresh1", tag="fresh0")
-        nc.vector.scalar_tensor_tensor(
-            out=fresh1[:, first], in0=v1[0][:], scalar=0.0, in1=gate1[:, first], op0=ALU.max, op1=ALU.mult
-        )
+        old1_lead = keep.tile([P, T // 4], F32, name="old1_lead", tag="lead")
+        nc.vector.tensor_copy(out=old1_lead[:], in_=windows[1][:].indirect(entries(lead)))
         nc.vector.tensor_copy(out=windows[0][:].indirect(entries(tail)), in_=new0[:, tail])
         nc.sync.dma_start(out=out[0:P, :], in_=windows[0][:])
-        nc.gpsimd.tensor_tensor(out=fresh1[:, second], in0=cand1[:], in1=gate1[:, second], op=ALU.mult)
-        nc.gpsimd.tensor_tensor(out=kept1[:], in0=old1[:], in1=rest1, op=ALU.mult)
+        nc.gpsimd.tensor_tensor(out=fresh1[:], in0=cand1[:], in1=gate1, op=ALU.mult)
+        nc.gpsimd.tensor_tensor(out=kept1[:, tail], in0=old1[:], in1=rest1[:, tail], op=ALU.mult)
+        nc.gpsimd.tensor_tensor(out=kept1[:, lead], in0=old1_lead[:], in1=rest1[:, lead], op=ALU.mult)
         nc.vector.tensor_tensor(out=windows[1][:].indirect(offsets[:]), in0=kept1[:], in1=fresh1[:], op=ALU.add)
         nc.sync.dma_start(out=out[P : 2 * P, :], in_=windows[1][:])

@@ -65,7 +65,7 @@ def tile_picked_wgmem_relu_l_kernel(tc, x_words, x_scales, mem, w1, w2, slot, ou
                 nc.vector.tensor_copy(out=dst, in_=src)
 
         def quantise(name, b):
-            codes[name, b] = keep.tile([P, P], U32, name="codes_%s%d" % (name, b), align_bytes=64)
+            codes[name, b] = keep.tile([P, P], U32, name="codes_%s%d" % (name, b), tag="codes_%s%d" % (name, b), align_bytes=64)
             planes[name, b] = keep.tile([P, P], U8, name="plane_%s%d" % (name, b), align_bytes=64)
             nc.vector.quantize_mx(
                 out=codes[name, b][:].bitcast(FP8X4),
@@ -73,11 +73,14 @@ def tile_picked_wgmem_relu_l_kernel(tc, x_words, x_scales, mem, w1, w2, slot, ou
                 in_=grouped[name, b][:].rearrange("p m j -> p (m j)"),
             )
 
-        def product(name, b, cols):
+        def product(name, b, cols, target=None):
             width = cols.stop - cols.start
-            acc = psum.tile([P, width], F32, name="acc_%s%d_%d" % (name, b, cols.start))
+            acc = None
+            if target is None:
+                acc = psum.tile([P, width], F32, name="acc_%s%d_%d" % (name, b, cols.start))
+                target = acc[:]
             nc.tensor.matmul_mx(
-                out=acc[:],
+                out=target,
                 lhsT=codes[name, b][:].bitcast(FP8X4),
                 lhsT_scale=planes[name, b][:],
                 rhs=x_codes[:, cols].bitcast(FP8X4),
@@ -102,8 +105,8 @@ def tile_picked_wgmem_relu_l_kernel(tc, x_words, x_scales, mem, w1, w2, slot, ou
         first, second = halves
         kept0, fresh0 = wide("kept0"), wide("fresh0")
         lead, tail = slice(0, T // 4), slice(T // 4, T)
-        fresh0_lead = keep.tile([P, T // 4], F32, name="fresh0_lead", tag="lead")
-        old1 = keep.tile([P, T - T // 4], F32, name="old1")
+        old1 = wide("old1")
+        fresh0_lead = old1[:, lead]
         rest0, gate0 = wide("rest0"), wide("gate0")
         u0 = {cols.start: product("gate", 0, cols) for cols in halves}
         v0 = {cols.start: product("cand", 0, cols) for cols in halves}
@@ -112,7 +115,7 @@ def tile_picked_wgmem_relu_l_kernel(tc, x_words, x_scales, mem, w1, w2, slot, ou
         for cols in halves:
             nc.scalar.activation(out=rest0[:, cols], in_=u0[cols.start][:], func=ACT.Sigmoid, scale=-1.0)
         for cols, bank, target in (
-            (lead, v0[0][:, lead], fresh0_lead[:]),
+            (lead, v0[0][:, lead], fresh0_lead),
             (slice(T // 4, T // 2), v0[0][:, T // 4 :], fresh0[:, T // 4 : T // 2]),
             (second, v0[T // 2][:], fresh0[:, second]),
         ):
@@ -124,25 +127,30 @@ def tile_picked_wgmem_relu_l_kernel(tc, x_words, x_scales, mem, w1, w2, slot, ou
         u1 = product("gate", 1, every)
         cast("cand", 1, True)
         quantise("cand", 1)
-        nc.vector.tensor_copy(out=old1[:], in_=windows[1][:].indirect(entries(tail)))
+        nc.vector.tensor_copy(out=old1[:, tail], in_=windows[1][:].indirect(entries(tail)))
         new0 = keep.tile([P, T], F32, name="new0", tag="grouped_cand1", align_bytes=64)
-        nc.gpsimd.tensor_tensor(out=new0[:, lead], in0=kept0[:, lead], in1=fresh0_lead[:], op=ALU.add)
+        nc.gpsimd.tensor_tensor(out=new0[:, lead], in0=kept0[:, lead], in1=fresh0_lead, op=ALU.add)
         nc.gpsimd.tensor_tensor(out=new0[:, tail], in0=kept0[:, tail], in1=fresh0[:, tail], op=ALU.add)
-        v1 = product("cand", 1, every)
+        v1_lead = product("cand", 1, lead)
+        v1 = psum.tile([P, T], F32, name="acc_cand1_tail")
+        for cols in (slice(T // 4, T // 2), second):
+            product("cand", 1, cols, v1[:, cols])
         kept1 = wide("kept1")
-        sigmoids1 = keep.tile([P, 2 * T], F32, name="sigmoids1", tag="raw_cand1")
-        gate1, rest1 = sigmoids1[:, :T], sigmoids1[:, T:]
+        gate1_tile = keep.tile([P, T], F32, name="gate1", tag="raw_cand1")
+        rest1_tile = keep.tile([P, T], F32, name="rest1", tag="codes_cand1", align_bytes=64)
+        gate1, rest1 = gate1_tile[:], rest1_tile[:]
         cand1, fresh1 = wide("cand1"), wide("fresh1")
         nc.scalar.activation(out=gate1, in_=u1[:], func=ACT.Sigmoid)
+        nc.scalar.activation(out=cand1[:, tail], in_=v1[:, tail], func=ACT.Relu)
         nc.scalar.activation(out=rest1, in_=u1[:], func=ACT.Sigmoid, scale=-1.0)
-        nc.scalar.activation(out=cand1[:], in_=v1[:], func=ACT.Relu)
         nc.vector.tensor_copy(out=windows[0][:].indirect(entries(lead)), in_=new0[:, lead])
-        old1_lead = keep.tile([P, T // 4], F32, name="old1_lead", tag="lead")
-        nc.vector.tensor_copy(out=old1_lead[:], in_=windows[1][:].indirect(entries(lead)))
+        nc.vector.tensor_copy(out=old1[:, lead], in_=windows[1][:].indirect(entries(lead)))
+        nc.vector.scalar_tensor_tensor(
+            out=fresh1[:, lead], in0=v1_lead[:], scalar=0.0, in1=gate1[:, lead], op0=ALU.max, op1=ALU.mult
+        )
         nc.vector.tensor_copy(out=windows[0][:].indirect(entries(tail)), in_=new0[:, tail])
         nc.sync.dma_start(out=out[0:P, :], in_=windows[0][:])
-        nc.gpsimd.tensor_tensor(out=fresh1[:], in0=cand1[:], in1=gate1, op=ALU.mult)
-        nc.gpsimd.tensor_tensor(out=kept1[:, tail], in0=old1[:], in1=rest1[:, tail], op=ALU.mult)
-        nc.gpsimd.tensor_tensor(out=kept1[:, lead], in0=old1_lead[:], in1=rest1[:, lead], op=ALU.mult)
+        nc.gpsimd.tensor_tensor(out=fresh1[:, tail], in0=cand1[:, tail], in1=gate1[:, tail], op=ALU.mult)
+        nc.gpsimd.tensor_tensor(out=kept1[:], in0=old1[:], in1=rest1, op=ALU.mult)
         nc.vector.tensor_tensor(out=windows[1][:].indirect(offsets[:]), in0=kept1[:], in1=fresh1[:], op=ALU.add)
         nc.sync.dma_start(out=out[P : 2 * P, :], in_=windows[1][:])

@@ -15,6 +15,9 @@ ACT = mybir.ActivationFunctionType
 P = 128
 PACK = 4
 K, T, N, U = 512, 512, 256, 1024
+LIST_ROWS = 16
+RUN = 4
+QUARTER = T // 4
 FLOPS = 2 * 2 * K * N * T
 
 
@@ -24,7 +27,7 @@ def tile_picked_wgmem_relu_l_kernel(tc, x_words, x_scales, mem, w1, w2, slot, ou
         keep = ctx.enter_context(tc.tile_pool(name="keep", bufs=1))
         psum = ctx.enter_context(tc.psum_pool(name="psum", bufs=1))
 
-        offsets = keep.tile([P, T // 16], U16, name="offsets")
+        offsets = keep.tile([P, T // LIST_ROWS], U16, name="offsets")
         x_codes = keep.tile([P, T], U32, name="x_codes", align_bytes=64)
         x_plane = keep.tile([P, T], U8, name="x_plane", align_bytes=64)
         windows = [keep.tile([P, U], F32, name="window%d" % b) for b in range(2)]
@@ -53,32 +56,23 @@ def tile_picked_wgmem_relu_l_kernel(tc, x_words, x_scales, mem, w1, w2, slot, ou
 
         codes = {}
         planes = {}
-        grouped = {}
 
-        def cast(name, b, on_scalar):
-            grouped[name, b] = keep.tile([P, P, PACK], BF16, name="grouped_%s%d" % (name, b), tag="grouped_%s%d" % (name, b), align_bytes=64)
-            src = raw[name, b][:].rearrange("p j (c i) -> p c j i", i=4)
-            dst = grouped[name, b][:].rearrange("p (c i) j -> p c j i", i=4)
-            if on_scalar:
-                nc.scalar.copy(out=dst, in_=src)
-            else:
-                nc.vector.tensor_copy(out=dst, in_=src)
-
-        def quantise(name, b):
-            codes[name, b] = keep.tile([P, P], U32, name="codes_%s%d" % (name, b), tag="codes_%s%d" % (name, b), align_bytes=64)
-            planes[name, b] = keep.tile([P, P], U8, name="plane_%s%d" % (name, b), align_bytes=64)
+        def quantise(name, b, cast):
+            label = "%s%d" % (name, b)
+            grouped = keep.tile([P, P, PACK], BF16, name="grouped_" + label, tag="grouped_" + label, align_bytes=64)
+            cast(
+                out=grouped[:].rearrange("p (c i) j -> p c j i", i=RUN),
+                in_=raw[name, b][:].rearrange("p j (c i) -> p c j i", i=RUN),
+            )
+            codes[name, b] = keep.tile([P, P], U32, name="codes_" + label, tag="codes_" + label, align_bytes=64)
+            planes[name, b] = keep.tile([P, P], U8, name="plane_" + label, align_bytes=64)
             nc.vector.quantize_mx(
                 out=codes[name, b][:].bitcast(FP8X4),
                 scales=planes[name, b][:],
-                in_=grouped[name, b][:].rearrange("p m j -> p (m j)"),
+                in_=grouped[:].rearrange("p m j -> p (m j)"),
             )
 
-        def product(name, b, cols, target=None):
-            width = cols.stop - cols.start
-            acc = None
-            if target is None:
-                acc = psum.tile([P, width], F32, name="acc_%s%d_%d" % (name, b, cols.start))
-                target = acc[:]
+        def multiply(target, name, b, cols):
             nc.tensor.matmul_mx(
                 out=target,
                 lhsT=codes[name, b][:].bitcast(FP8X4),
@@ -88,69 +82,70 @@ def tile_picked_wgmem_relu_l_kernel(tc, x_words, x_scales, mem, w1, w2, slot, ou
                 start=True,
                 stop=True,
             )
-            return acc
+
+        def product(name, b, cols):
+            bank = psum.tile([P, cols.stop - cols.start], F32, name="bank_%s%d_%d" % (name, b, cols.start))
+            multiply(bank[:], name, b, cols)
+            return bank
 
         def entries(cols):
-            return offsets[:, cols.start // 16 : cols.stop // 16]
+            return offsets[:, cols.start // LIST_ROWS : cols.stop // LIST_ROWS]
 
-        def wide(name):
-            return keep.tile([P, T], F32, name=name, tag=name)
+        def per_message(name):
+            return keep.tile([P, T], F32, name=name)
 
-        every = slice(0, T)
+        def relu_times(target, bank, gate):
+            nc.vector.scalar_tensor_tensor(out=target, in0=bank, scalar=0.0, in1=gate, op0=ALU.max, op1=ALU.mult)
+
+        halves = [slice(0, T // 2), slice(T // 2, T)]
+        lead, tail = slice(0, QUARTER), slice(QUARTER, T)
+        early, last = slice(0, T - QUARTER), slice(T - QUARTER, T)
 
         for name, b in (("gate", 0), ("cand", 0), ("gate", 1)):
-            cast(name, b, False)
-            quantise(name, b)
-        halves = [slice(0, T // 2), slice(T // 2, T)]
-        first, second = halves
-        kept0, fresh0 = wide("kept0"), wide("fresh0")
-        lead, tail = slice(0, T // 4), slice(T // 4, T)
-        old1 = wide("old1")
-        fresh0_lead = old1[:, lead]
-        rest0, gate0 = wide("rest0"), wide("gate0")
-        u0 = {cols.start: product("gate", 0, cols) for cols in halves}
-        v0 = {cols.start: product("cand", 0, cols) for cols in halves}
-        for cols in halves:
-            nc.scalar.activation(out=gate0[:, cols], in_=u0[cols.start][:], func=ACT.Sigmoid)
-        for cols in halves:
-            nc.scalar.activation(out=rest0[:, cols], in_=u0[cols.start][:], func=ACT.Sigmoid, scale=-1.0)
-        for cols, bank, target in (
-            (lead, v0[0][:, lead], fresh0_lead),
-            (slice(T // 4, T // 2), v0[0][:, T // 4 :], fresh0[:, T // 4 : T // 2]),
-            (second, v0[T // 2][:], fresh0[:, second]),
-        ):
-            nc.vector.scalar_tensor_tensor(out=target, in0=bank, scalar=0.0, in1=gate0[:, cols], op0=ALU.max, op1=ALU.mult)
+            quantise(name, b, nc.vector.tensor_copy)
+
+        shared = keep.tile([P, 2 * T - QUARTER], F32, name="shared")
+        old1, kept0 = shared[:, :T], shared[:, T - QUARTER :]
+        fresh0, rest0, gate0 = per_message("fresh0"), per_message("rest0"), per_message("gate0")
+        u0 = [product("gate", 0, cols) for cols in halves]
+        v0 = [product("cand", 0, cols) for cols in halves]
+        for cols, bank in zip(halves, u0):
+            nc.scalar.activation(out=gate0[:, cols], in_=bank[:], func=ACT.Sigmoid)
+        for cols, bank in zip(halves, u0):
+            nc.scalar.activation(out=rest0[:, cols], in_=bank[:], func=ACT.Sigmoid, scale=-1.0)
+        for cols, bank in zip(halves, v0):
+            relu_times(fresh0[:, cols], bank[:], gate0[:, cols])
         for cols in halves:
             nc.vector.tensor_tensor(
                 out=kept0[:, cols], in0=windows[0][:].indirect(entries(cols)), in1=rest0[:, cols], op=ALU.mult
             )
-        u1 = product("gate", 1, every)
-        cast("cand", 1, True)
-        quantise("cand", 1)
-        nc.vector.tensor_copy(out=old1[:, tail], in_=windows[1][:].indirect(entries(tail)))
+        u1 = product("gate", 1, slice(0, T))
+
+        quantise("cand", 1, nc.scalar.copy)
+        nc.vector.tensor_copy(out=old1[:, early], in_=windows[1][:].indirect(entries(early)))
+
         new0 = keep.tile([P, T], F32, name="new0", tag="grouped_cand1", align_bytes=64)
-        nc.gpsimd.tensor_tensor(out=new0[:, lead], in0=kept0[:, lead], in1=fresh0_lead, op=ALU.add)
-        nc.gpsimd.tensor_tensor(out=new0[:, tail], in0=kept0[:, tail], in1=fresh0[:, tail], op=ALU.add)
+        gate1 = keep.tile([P, T], F32, name="gate1", tag="raw_cand1")
+        for cols in (lead, tail):
+            nc.gpsimd.tensor_tensor(out=new0[:, cols], in0=kept0[:, cols], in1=fresh0[:, cols], op=ALU.add)
+
         v1_lead = product("cand", 1, lead)
-        v1 = psum.tile([P, T], F32, name="acc_cand1_tail")
-        for cols in (slice(T // 4, T // 2), second):
-            product("cand", 1, cols, v1[:, cols])
-        kept1 = wide("kept1")
-        gate1_tile = keep.tile([P, T], F32, name="gate1", tag="raw_cand1")
-        rest1_tile = keep.tile([P, T], F32, name="rest1", tag="codes_cand1", align_bytes=64)
-        gate1, rest1 = gate1_tile[:], rest1_tile[:]
-        cand1, fresh1 = wide("cand1"), wide("fresh1")
-        nc.scalar.activation(out=gate1, in_=u1[:], func=ACT.Sigmoid)
-        nc.scalar.activation(out=cand1[:, tail], in_=v1[:, tail], func=ACT.Relu)
-        nc.scalar.activation(out=rest1, in_=u1[:], func=ACT.Sigmoid, scale=-1.0)
+        v1_tail = psum.tile([P, T], F32, name="bank_cand1_tail")
+        for cols in (slice(QUARTER, T // 2), halves[1]):
+            multiply(v1_tail[:, cols], "cand", 1, cols)
+        rest1 = keep.tile([P, T], F32, name="rest1", tag="codes_cand1", align_bytes=64)
+        kept1, cand1, fresh1 = per_message("kept1"), per_message("cand1"), per_message("fresh1")
+        nc.scalar.activation(out=gate1[:], in_=u1[:], func=ACT.Sigmoid)
+        nc.scalar.activation(out=cand1[:, tail], in_=v1_tail[:, tail], func=ACT.Relu)
+        nc.scalar.activation(out=rest1[:], in_=u1[:], func=ACT.Sigmoid, scale=-1.0)
+
         nc.vector.tensor_copy(out=windows[0][:].indirect(entries(lead)), in_=new0[:, lead])
-        nc.vector.tensor_copy(out=old1[:, lead], in_=windows[1][:].indirect(entries(lead)))
-        nc.vector.scalar_tensor_tensor(
-            out=fresh1[:, lead], in0=v1_lead[:], scalar=0.0, in1=gate1[:, lead], op0=ALU.max, op1=ALU.mult
-        )
+        nc.vector.tensor_copy(out=old1[:, last], in_=windows[1][:].indirect(entries(last)))
+        relu_times(fresh1[:, lead], v1_lead[:], gate1[:, lead])
         nc.vector.tensor_copy(out=windows[0][:].indirect(entries(tail)), in_=new0[:, tail])
         nc.sync.dma_start(out=out[0:P, :], in_=windows[0][:])
+
         nc.gpsimd.tensor_tensor(out=fresh1[:, tail], in0=cand1[:, tail], in1=gate1[:, tail], op=ALU.mult)
-        nc.gpsimd.tensor_tensor(out=kept1[:], in0=old1[:], in1=rest1, op=ALU.mult)
+        nc.gpsimd.tensor_tensor(out=kept1[:], in0=old1, in1=rest1[:], op=ALU.mult)
         nc.vector.tensor_tensor(out=windows[1][:].indirect(offsets[:]), in0=kept1[:], in1=fresh1[:], op=ALU.add)
         nc.sync.dma_start(out=out[P : 2 * P, :], in_=windows[1][:])

@@ -39,7 +39,6 @@ def tile_picked_wgmem_relu_l_kernel(tc, x_words, x_scales, mem, w1, w2, slot, ou
         def load_weights(name, w, b):
             nc.sync.dma_start(out=raw[name, b][:], in_=w[:, b * P : (b + 1) * P].rearrange("(p j) m -> p j m", j=PACK))
 
-        nc.vector.memset(x_plane[:].bitcast(I32), 0)
         load_weights("gate", w2, 0)
         load_weights("cand", w1, 0)
         for q in range(4):

@@ -40,12 +40,14 @@ def tile_picked_wgmem_relu_l_kernel(tc, x_words, x_scales, mem, w1, w2, slot, ou
             nc.sync.dma_start(out=raw[name, b][:], in_=w[:, b * P : (b + 1) * P].rearrange("(p j) m -> p j m", j=PACK))
 
         load_weights("gate", w2, 0)
-        load_weights("cand", w1, 0)
-        for q in range(4):
-            nc.sync.dma_start(
-                out=x_plane[32 * q : 32 * q + 4, :].bitcast(I32),
-                in_=x_scales[0, 4 * q : 4 * q + 4, :].bitcast(I32),
-            )
+        for quadrants in ((0, 1), (2, 3)):
+            for q in quadrants:
+                nc.sync.dma_start(
+                    out=x_plane[32 * q : 32 * q + 4, :].bitcast(I32),
+                    in_=x_scales[0, 4 * q : 4 * q + 4, :].bitcast(I32),
+                )
+            if quadrants == (0, 1):
+                load_weights("cand", w1, 0)
         nc.sync.dma_start(out=x_codes[:].bitcast(I32), in_=x_words[0].rearrange("p n t -> p (n t)").bitcast(I32))
         load_weights("gate", w2, 1)
         nc.sync.dma_start(out=windows[0][:], in_=mem[0:P, :])

@@ -39,15 +39,16 @@ def tile_picked_wgmem_relu_l_kernel(tc, x_words, x_scales, mem, w1, w2, slot, ou
         def load_weights(name, w, b):
             nc.sync.dma_start(out=raw[name, b][:], in_=w[:, b * P : (b + 1) * P].rearrange("(p j) m -> p j m", j=PACK))
 
-        load_weights("gate", w2, 0)
-        for quadrants in ((0, 1), (2, 3)):
+        def load_scales(q):
+            nc.sync.dma_start(
+                out=x_plane[32 * q : 32 * q + 4, :].bitcast(I32),
+                in_=x_scales[0, 4 * q : 4 * q + 4, :].bitcast(I32),
+            )
+
+        for name, w, quadrants in (("gate", w2, (0, 1)), ("cand", w1, (2, 3))):
+            load_weights(name, w, 0)
             for q in quadrants:
-                nc.sync.dma_start(
-                    out=x_plane[32 * q : 32 * q + 4, :].bitcast(I32),
-                    in_=x_scales[0, 4 * q : 4 * q + 4, :].bitcast(I32),
-                )
-            if quadrants == (0, 1):
-                load_weights("cand", w1, 0)
+                load_scales(q)
         nc.sync.dma_start(out=x_codes[:].bitcast(I32), in_=x_words[0].rearrange("p n t -> p (n t)").bitcast(I32))
         load_weights("gate", w2, 1)
         nc.sync.dma_start(out=windows[0][:], in_=mem[0:P, :])
@@ -99,14 +100,17 @@ def tile_picked_wgmem_relu_l_kernel(tc, x_words, x_scales, mem, w1, w2, slot, ou
             nc.vector.scalar_tensor_tensor(out=target, in0=bank, scalar=0.0, in1=gate, op0=ALU.max, op1=ALU.mult)
 
         halves = [slice(0, T // 2), slice(T // 2, T)]
-        lead, tail = slice(0, QUARTER), slice(QUARTER, T)
+        first, others = slice(0, QUARTER), slice(QUARTER, T)
         early, last = slice(0, T - QUARTER), slice(T - QUARTER, T)
+        joined = slice(0, T + QUARTER)
 
         for name, b in (("gate", 0), ("cand", 0), ("gate", 1)):
             quantise(name, b, nc.vector.tensor_copy)
 
-        shared = keep.tile([P, 2 * T - QUARTER], F32, name="shared")
-        old1, kept0 = shared[:, :T], shared[:, T - QUARTER :]
+        values, terms = (keep.tile([P, 2 * T], F32, name=n) for n in ("values", "terms"))
+        cand1, old1 = values[:, :T], values[:, T:]
+        fresh1, kept1 = terms[:, :T], terms[:, T:]
+        kept0 = values[:, QUARTER : T + QUARTER]
         fresh0, rest0, gate0 = per_message("fresh0"), per_message("rest0"), per_message("gate0")
         u0 = [product("gate", 0, cols) for cols in halves]
         v0 = [product("cand", 0, cols) for cols in halves]
@@ -123,30 +127,25 @@ def tile_picked_wgmem_relu_l_kernel(tc, x_words, x_scales, mem, w1, w2, slot, ou
         u1 = product("gate", 1, slice(0, T))
 
         quantise("cand", 1, nc.scalar.copy)
-        nc.vector.tensor_copy(out=old1[:, early], in_=windows[1][:].indirect(entries(early)))
+        nc.vector.tensor_copy(out=old1[:, others], in_=windows[1][:].indirect(entries(others)))
 
         new0 = keep.tile([P, T], F32, name="new0", tag="grouped_cand1", align_bytes=64)
-        gate1 = keep.tile([P, T], F32, name="gate1", tag="raw_cand1")
-        for cols in (lead, tail):
+        factors = keep.tile([P, 2 * T], F32, name="factors", tag="raw_cand1")
+        gate1, rest1 = factors[:, :T], factors[:, T:]
+        for cols in (last, early):
             nc.gpsimd.tensor_tensor(out=new0[:, cols], in0=kept0[:, cols], in1=fresh0[:, cols], op=ALU.add)
 
-        v1_lead = product("cand", 1, lead)
-        v1_tail = psum.tile([P, T], F32, name="bank_cand1_tail")
-        for cols in (slice(QUARTER, T // 2), halves[1]):
-            multiply(v1_tail[:, cols], "cand", 1, cols)
-        rest1 = keep.tile([P, T], F32, name="rest1", tag="codes_cand1", align_bytes=64)
-        kept1, cand1, fresh1 = per_message("kept1"), per_message("cand1"), per_message("fresh1")
-        nc.scalar.activation(out=gate1[:], in_=u1[:], func=ACT.Sigmoid)
-        nc.scalar.activation(out=cand1[:, tail], in_=v1_tail[:, tail], func=ACT.Relu)
-        nc.scalar.activation(out=rest1[:], in_=u1[:], func=ACT.Sigmoid, scale=-1.0)
+        v1 = product("cand", 1, slice(0, T))
+        nc.scalar.activation(out=rest1, in_=u1[:], func=ACT.Sigmoid, scale=-1.0)
+        nc.scalar.activation(out=gate1, in_=u1[:], func=ACT.Sigmoid)
+        nc.scalar.activation(out=cand1, in_=v1[:], func=ACT.Relu)
 
-        nc.vector.tensor_copy(out=windows[0][:].indirect(entries(lead)), in_=new0[:, lead])
-        nc.vector.tensor_copy(out=old1[:, last], in_=windows[1][:].indirect(entries(last)))
-        relu_times(fresh1[:, lead], v1_lead[:], gate1[:, lead])
-        nc.vector.tensor_copy(out=windows[0][:].indirect(entries(tail)), in_=new0[:, tail])
+        nc.vector.tensor_copy(out=windows[0][:].indirect(entries(last)), in_=new0[:, last])
+        nc.vector.tensor_copy(out=old1[:, first], in_=windows[1][:].indirect(entries(first)))
+        nc.vector.tensor_copy(out=windows[0][:].indirect(entries(early)), in_=new0[:, early])
         nc.sync.dma_start(out=out[0:P, :], in_=windows[0][:])
 
-        nc.gpsimd.tensor_tensor(out=fresh1[:, tail], in0=cand1[:, tail], in1=gate1[:, tail], op=ALU.mult)
-        nc.gpsimd.tensor_tensor(out=kept1[:], in0=old1, in1=rest1[:], op=ALU.mult)
-        nc.vector.tensor_tensor(out=windows[1][:].indirect(offsets[:]), in0=kept1[:], in1=fresh1[:], op=ALU.add)
+        nc.gpsimd.tensor_tensor(out=kept1[:, others], in0=old1[:, others], in1=rest1[:, others], op=ALU.mult)
+        nc.gpsimd.tensor_tensor(out=terms[:, joined], in0=values[:, joined], in1=factors[:, joined], op=ALU.mult)
+        nc.vector.tensor_tensor(out=windows[1][:].indirect(offsets[:]), in0=kept1, in1=fresh1, op=ALU.add)
         nc.sync.dma_start(out=out[P : 2 * P, :], in_=windows[1][:])

@@ -17,7 +17,7 @@ PACK = 4
 K, T, N, U = 512, 512, 256, 1024
 LIST_ROWS = 16
 RUN = 4
-QUARTER = T // 4
+QUADRANTS = 4
 FLOPS = 2 * 2 * K * N * T
 
 
@@ -29,54 +29,68 @@ def tile_picked_wgmem_relu_l_kernel(tc, x_words, x_scales, mem, w1, w2, slot, ou
 
         offsets = keep.tile([P, T // LIST_ROWS], U16, name="offsets")
         x_codes = keep.tile([P, T], U32, name="x_codes", align_bytes=64)
-        x_plane = keep.tile([P, T], U8, name="x_plane", align_bytes=64)
-        windows = [keep.tile([P, U], F32, name="window%d" % b) for b in range(2)]
+        x_scale_rows = keep.tile([P, QUADRANTS, T], U8, name="x_scale_rows", align_bytes=64)
+        x_plane = x_scale_rows[:, 0, :]
+        windows = [keep.tile([P, U], F32, name="window%d" % b, align_bytes=256) for b in range(2)]
         raw = {}
         for b in range(2):
             for name in ("gate", "cand"):
-                raw[name, b] = keep.tile([P, PACK, P], F32, name="raw_%s%d" % (name, b), tag="raw_%s%d" % (name, b))
+                raw[name, b] = keep.tile(
+                    [P, PACK, P], F32, name="raw_%s%d" % (name, b), tag="raw_%s%d" % (name, b), align_bytes=256
+                )
 
         def load_weights(name, w, b):
             nc.sync.dma_start(out=raw[name, b][:], in_=w[:, b * P : (b + 1) * P].rearrange("(p j) m -> p j m", j=PACK))
 
-        def load_scales(q):
+        def load_scales():
             nc.sync.dma_start(
-                out=x_plane[32 * q : 32 * q + 4, :].bitcast(I32),
-                in_=x_scales[0, 4 * q : 4 * q + 4, :].bitcast(I32),
+                out=x_scale_rows[0:4, :, :].bitcast(I32),
+                in_=x_scales[0].rearrange("(q r) c -> r q c", q=QUADRANTS).bitcast(I32),
             )
 
-        for name, w, quadrants in (("gate", w2, (0, 1)), ("cand", w1, (2, 3))):
-            load_weights(name, w, 0)
-            for q in quadrants:
-                load_scales(q)
-        nc.sync.dma_start(out=x_codes[:].bitcast(I32), in_=x_words[0].rearrange("p n t -> p (n t)").bitcast(I32))
-        load_weights("gate", w2, 1)
-        nc.sync.dma_start(out=windows[0][:], in_=mem[0:P, :])
-        nc.sync.dma_start(offsets[:], slot)
-        load_weights("cand", w1, 1)
-        nc.sync.dma_start(out=windows[1][:], in_=mem[P : 2 * P, :])
+        def spread_scales():
+            for q in range(1, QUADRANTS):
+                nc.vector.tensor_copy(
+                    out=x_scale_rows[32 * q : 32 * q + 4, 0, :].bitcast(I32), in_=x_scale_rows[0:4, q, :].bitcast(I32)
+                )
+
+        def load_codes():
+            nc.sync.dma_start(out=x_codes[:].bitcast(I32), in_=x_words[0].rearrange("p n t -> p (n t)").bitcast(I32))
+
+        def load_window(b):
+            nc.sync.dma_start(out=windows[b][:], in_=mem[b * P : (b + 1) * P, :])
+
+        def store_window(b):
+            nc.sync.dma_start(out=out[b * P : (b + 1) * P, :], in_=windows[b][:])
 
         codes = {}
         planes = {}
+        grouped = {}
 
-        def quantise(name, b, cast):
+        def cast(name, b, copy):
             label = "%s%d" % (name, b)
-            grouped = keep.tile([P, P, PACK], BF16, name="grouped_" + label, tag="grouped_" + label, align_bytes=64)
-            cast(
-                out=grouped[:].rearrange("p (c i) j -> p c j i", i=RUN),
+            grouped[name, b] = keep.tile(
+                [P, P, PACK], BF16, name="grouped_" + label, tag="grouped_" + label, align_bytes=64
+            )
+            copy(
+                out=grouped[name, b][:].rearrange("p (c i) j -> p c j i", i=RUN),
                 in_=raw[name, b][:].rearrange("p j (c i) -> p c j i", i=RUN),
             )
+
+        def quantise(name, b):
+            label = "%s%d" % (name, b)
             codes[name, b] = keep.tile([P, P], U32, name="codes_" + label, tag="codes_" + label, align_bytes=64)
             planes[name, b] = keep.tile([P, P], U8, name="plane_" + label, align_bytes=64)
             nc.vector.quantize_mx(
                 out=codes[name, b][:].bitcast(FP8X4),
                 scales=planes[name, b][:],
-                in_=grouped[:].rearrange("p m j -> p (m j)"),
+                in_=grouped[name, b][:].rearrange("p m j -> p (m j)"),
             )
 
-        def multiply(target, name, b, cols):
+        def product(name, b, cols):
+            bank = psum.tile([P, cols.stop - cols.start], F32, name="bank_%s%d_%d" % (name, b, cols.start))
             nc.tensor.matmul_mx(
-                out=target,
+                out=bank[:],
                 lhsT=codes[name, b][:].bitcast(FP8X4),
                 lhsT_scale=planes[name, b][:],
                 rhs=x_codes[:, cols].bitcast(FP8X4),
@@ -84,68 +98,72 @@ def tile_picked_wgmem_relu_l_kernel(tc, x_words, x_scales, mem, w1, w2, slot, ou
                 start=True,
                 stop=True,
             )
-
-        def product(name, b, cols):
-            bank = psum.tile([P, cols.stop - cols.start], F32, name="bank_%s%d_%d" % (name, b, cols.start))
-            multiply(bank[:], name, b, cols)
             return bank
 
-        def entries(cols):
-            return offsets[:, cols.start // LIST_ROWS : cols.stop // LIST_ROWS]
+        def picked(b, cols):
+            return windows[b][:].indirect(offsets[:, cols.start // LIST_ROWS : cols.stop // LIST_ROWS])
 
         def per_message(name):
-            return keep.tile([P, T], F32, name=name)
+            return keep.tile([P, T], F32, name=name, tag=name, align_bytes=64)
 
         def relu_times(target, bank, gate):
             nc.vector.scalar_tensor_tensor(out=target, in0=bank, scalar=0.0, in1=gate, op0=ALU.max, op1=ALU.mult)
 
+        def sigmoid(target, bank, sign):
+            nc.scalar.activation(out=target, in_=bank, func=ACT.Sigmoid, scale=sign)
+
+        whole = slice(0, T)
         halves = [slice(0, T // 2), slice(T // 2, T)]
-        first, others = slice(0, QUARTER), slice(QUARTER, T)
-        early, last = slice(0, T - QUARTER), slice(T - QUARTER, T)
-        joined = slice(0, T + QUARTER)
 
-        for name, b in (("gate", 0), ("cand", 0), ("gate", 1)):
-            quantise(name, b, nc.vector.tensor_copy)
+        load_weights("gate", w2, 0)
+        load_scales()
+        load_weights("cand", w1, 0)
+        load_codes()
+        nc.sync.dma_start(offsets[:], slot)
+        load_weights("gate", w2, 1)
+        load_weights("cand", w1, 1)
+        load_window(0)
+        load_window(1)
 
-        values, terms = (keep.tile([P, 2 * T], F32, name=n) for n in ("values", "terms"))
-        cand1, old1 = values[:, :T], values[:, T:]
-        fresh1, kept1 = terms[:, :T], terms[:, T:]
-        kept0 = values[:, QUARTER : T + QUARTER]
-        fresh0, rest0, gate0 = per_message("fresh0"), per_message("rest0"), per_message("gate0")
+        cast("gate", 0, nc.vector.tensor_copy)
+        spread_scales()
+        quantise("gate", 0)
+        for name, b in (("cand", 0), ("gate", 1), ("cand", 1)):
+            cast(name, b, nc.vector.tensor_copy)
+            quantise(name, b)
+
+        first, second = halves
+        gate0, rest0, gate1, rest1 = (per_message(n) for n in ("gate0", "rest0", "gate1", "rest1"))
+        fresh0, fresh1 = per_message("fresh0"), per_message("fresh1")
+        old0, kept0, new0, kept1 = (per_message(n) for n in ("old0", "kept0", "new0", "kept1"))
+
         u0 = [product("gate", 0, cols) for cols in halves]
         v0 = [product("cand", 0, cols) for cols in halves]
+        u1 = [product("gate", 1, cols) for cols in halves]
+        v1 = [product("cand", 1, cols) for cols in halves]
         for cols, bank in zip(halves, u0):
-            nc.scalar.activation(out=gate0[:, cols], in_=bank[:], func=ACT.Sigmoid)
-        for cols, bank in zip(halves, u0):
-            nc.scalar.activation(out=rest0[:, cols], in_=bank[:], func=ACT.Sigmoid, scale=-1.0)
+            sigmoid(gate0[:, cols], bank[:], 1.0)
+        sigmoid(rest0[:, first], u0[0][:], -1.0)
         for cols, bank in zip(halves, v0):
             relu_times(fresh0[:, cols], bank[:], gate0[:, cols])
+
+        nc.vector.tensor_tensor(out=kept0[:, first], in0=picked(0, first), in1=rest0[:, first], op=ALU.mult)
+        for cols, bank in zip(halves, u1):
+            sigmoid(gate1[:, cols], bank[:], 1.0)
+        nc.scalar.activation(out=old0[:, second], in_=picked(0, second), func=ACT.Copy)
+        for cols, bank in zip(halves, u1):
+            sigmoid(rest1[:, cols], bank[:], -1.0)
+
+        nc.vector.tensor_tensor(out=new0[:, first], in0=kept0[:, first], in1=fresh0[:, first], op=ALU.add)
+        nc.vector.scalar_tensor_tensor(
+            out=kept0[:, second], in0=gate0[:, second], scalar=1.0, in1=old0[:, second], op0=ALU.subtract, op1=ALU.mult
+        )
+        for cols, bank in zip(halves, v1):
+            relu_times(fresh1[:, cols], bank[:], gate1[:, cols])
+        nc.vector.tensor_tensor(out=kept1[:], in0=picked(1, whole), in1=rest1[:], op=ALU.mult)
+        nc.vector.tensor_tensor(out=new0[:, second], in0=fresh0[:, second], in1=kept0[:, second], op=ALU.subtract)
         for cols in halves:
-            nc.vector.tensor_tensor(
-                out=kept0[:, cols], in0=windows[0][:].indirect(entries(cols)), in1=rest0[:, cols], op=ALU.mult
-            )
-        u1 = product("gate", 1, slice(0, T))
-
-        quantise("cand", 1, nc.scalar.copy)
-        nc.vector.tensor_copy(out=old1[:, others], in_=windows[1][:].indirect(entries(others)))
-
-        new0 = keep.tile([P, T], F32, name="new0", tag="grouped_cand1", align_bytes=64)
-        factors = keep.tile([P, 2 * T], F32, name="factors", tag="raw_cand1")
-        gate1, rest1 = factors[:, :T], factors[:, T:]
-        for cols in (last, early):
-            nc.gpsimd.tensor_tensor(out=new0[:, cols], in0=kept0[:, cols], in1=fresh0[:, cols], op=ALU.add)
-
-        v1 = product("cand", 1, slice(0, T))
-        nc.scalar.activation(out=rest1, in_=u1[:], func=ACT.Sigmoid, scale=-1.0)
-        nc.scalar.activation(out=gate1, in_=u1[:], func=ACT.Sigmoid)
-        nc.scalar.activation(out=cand1, in_=v1[:], func=ACT.Relu)
-
-        nc.vector.tensor_copy(out=windows[0][:].indirect(entries(last)), in_=new0[:, last])
-        nc.vector.tensor_copy(out=old1[:, first], in_=windows[1][:].indirect(entries(first)))
-        nc.vector.tensor_copy(out=windows[0][:].indirect(entries(early)), in_=new0[:, early])
-        nc.sync.dma_start(out=out[0:P, :], in_=windows[0][:])
-
-        nc.gpsimd.tensor_tensor(out=kept1[:, others], in0=old1[:, others], in1=rest1[:, others], op=ALU.mult)
-        nc.gpsimd.tensor_tensor(out=terms[:, joined], in0=values[:, joined], in1=factors[:, joined], op=ALU.mult)
-        nc.vector.tensor_tensor(out=windows[1][:].indirect(offsets[:]), in0=kept1, in1=fresh1, op=ALU.add)
-        nc.sync.dma_start(out=out[P : 2 * P, :], in_=windows[1][:])
+            nc.scalar.activation(out=picked(0, cols), in_=new0[:, cols], func=ACT.Copy)
+        store_window(0)
+        nc.vector.tensor_tensor(out=picked(1, whole), in0=kept1[:], in1=fresh1[:], op=ALU.add)
+        store_window(1)

@@ -17,7 +17,6 @@ PACK = 4
 K, T, N, U = 512, 512, 256, 1024
 LIST_ROWS = 16
 RUN = 4
-QUADRANTS = 4
 FLOPS = 2 * 2 * K * N * T
 
 
@@ -29,8 +28,7 @@ def tile_picked_wgmem_relu_l_kernel(tc, x_words, x_scales, mem, w1, w2, slot, ou
 
         offsets = keep.tile([P, T // LIST_ROWS], U16, name="offsets")
         x_codes = keep.tile([P, T], U32, name="x_codes", align_bytes=64)
-        x_scale_rows = keep.tile([P, QUADRANTS, T], U8, name="x_scale_rows", align_bytes=64)
-        x_plane = x_scale_rows[:, 0, :]
+        x_plane = keep.tile([P, T], U8, name="x_plane", align_bytes=64)
         windows = [keep.tile([P, U], F32, name="window%d" % b, align_bytes=256) for b in range(2)]
         raw = {}
         for b in range(2):
@@ -42,17 +40,11 @@ def tile_picked_wgmem_relu_l_kernel(tc, x_words, x_scales, mem, w1, w2, slot, ou
         def load_weights(name, w, b):
             nc.sync.dma_start(out=raw[name, b][:], in_=w[:, b * P : (b + 1) * P].rearrange("(p j) m -> p j m", j=PACK))
 
-        def load_scales():
+        def load_scales(q):
             nc.sync.dma_start(
-                out=x_scale_rows[0:4, :, :].bitcast(I32),
-                in_=x_scales[0].rearrange("(q r) c -> r q c", q=QUADRANTS).bitcast(I32),
+                out=x_plane[32 * q : 32 * q + 4, :].bitcast(I32),
+                in_=x_scales[0, 4 * q : 4 * q + 4, :].bitcast(I32),
             )
-
-        def spread_scales():
-            for q in range(1, QUADRANTS):
-                nc.vector.tensor_copy(
-                    out=x_scale_rows[32 * q : 32 * q + 4, 0, :].bitcast(I32), in_=x_scale_rows[0:4, q, :].bitcast(I32)
-                )
 
         def load_codes():
             nc.sync.dma_start(out=x_codes[:].bitcast(I32), in_=x_words[0].rearrange("p n t -> p (n t)").bitcast(I32))
@@ -116,17 +108,19 @@ def tile_picked_wgmem_relu_l_kernel(tc, x_words, x_scales, mem, w1, w2, slot, ou
         halves = [slice(0, T // 2), slice(T // 2, T)]
 
         load_weights("gate", w2, 0)
-        load_scales()
+        load_scales(0)
+        load_scales(1)
         load_weights("cand", w1, 0)
+        load_scales(2)
+        load_scales(3)
         load_codes()
-        nc.sync.dma_start(offsets[:], slot)
         load_weights("gate", w2, 1)
         load_weights("cand", w1, 1)
+        nc.sync.dma_start(offsets[:], slot)
         load_window(0)
         load_window(1)
 
         cast("gate", 0, nc.vector.tensor_copy)
-        spread_scales()
         quantise("gate", 0)
         for name, b in (("cand", 0), ("gate", 1), ("cand", 1)):
             cast(name, b, nc.vector.tensor_copy)

from contextlib import ExitStack

import concourse.mybir as mybir

F32 = mybir.dt.float32
BF16 = mybir.dt.bfloat16
I32 = mybir.dt.int32
U32 = mybir.dt.uint32
U16 = mybir.dt.uint16
U8 = mybir.dt.uint8
FP8X4 = mybir.dt.float8_e4m3fn_x4
ALU = mybir.AluOpType
ACT = mybir.ActivationFunctionType

P = 128
PACK = 4
K, T, N, U = 512, 512, 256, 1024
LIST_ROWS = 16
RUN = 4
FLOPS = 2 * 2 * K * N * T


def tile_picked_wgmem_relu_l_kernel(tc, x_words, x_scales, mem, w1, w2, slot, out):
    nc = tc.nc
    with ExitStack() as ctx:
        keep = ctx.enter_context(tc.tile_pool(name="keep", bufs=1))
        psum = ctx.enter_context(tc.psum_pool(name="psum", bufs=1))

        offsets = keep.tile([P, T // LIST_ROWS], U16, name="offsets")
        x_codes = keep.tile([P, T], U32, name="x_codes", align_bytes=64)
        x_plane = keep.tile([P, T], U8, name="x_plane", align_bytes=64)
        windows = [keep.tile([P, U], F32, name="window%d" % b, align_bytes=256) for b in range(2)]
        raw = {}
        for b in range(2):
            for name in ("gate", "cand"):
                raw[name, b] = keep.tile(
                    [P, PACK, P], F32, name="raw_%s%d" % (name, b), tag="raw_%s%d" % (name, b), align_bytes=256
                )

        def load_weights(name, w, b):
            nc.sync.dma_start(out=raw[name, b][:], in_=w[:, b * P : (b + 1) * P].rearrange("(p j) m -> p j m", j=PACK))

        def load_scales(q):
            nc.sync.dma_start(
                out=x_plane[32 * q : 32 * q + 4, :].bitcast(I32),
                in_=x_scales[0, 4 * q : 4 * q + 4, :].bitcast(I32),
            )

        def load_codes():
            nc.sync.dma_start(out=x_codes[:].bitcast(I32), in_=x_words[0].rearrange("p n t -> p (n t)").bitcast(I32))

        def load_window(b):
            nc.sync.dma_start(out=windows[b][:], in_=mem[b * P : (b + 1) * P, :])

        def store_window(b):
            nc.sync.dma_start(out=out[b * P : (b + 1) * P, :], in_=windows[b][:])

        codes = {}
        planes = {}
        grouped = {}

        def cast(name, b, copy):
            label = "%s%d" % (name, b)
            grouped[name, b] = keep.tile(
                [P, P, PACK], BF16, name="grouped_" + label, tag="grouped_" + label, align_bytes=64
            )
            copy(
                out=grouped[name, b][:].rearrange("p (c i) j -> p c j i", i=RUN),
                in_=raw[name, b][:].rearrange("p j (c i) -> p c j i", i=RUN),
            )

        def quantise(name, b):
            label = "%s%d" % (name, b)
            codes[name, b] = keep.tile([P, P], U32, name="codes_" + label, tag="codes_" + label, align_bytes=64)
            planes[name, b] = keep.tile([P, P], U8, name="plane_" + label, align_bytes=64)
            nc.vector.quantize_mx(
                out=codes[name, b][:].bitcast(FP8X4),
                scales=planes[name, b][:],
                in_=grouped[name, b][:].rearrange("p m j -> p (m j)"),
            )

        def product(name, b, cols):
            bank = psum.tile([P, cols.stop - cols.start], F32, name="bank_%s%d_%d" % (name, b, cols.start))
            nc.tensor.matmul_mx(
                out=bank[:],
                lhsT=codes[name, b][:].bitcast(FP8X4),
                lhsT_scale=planes[name, b][:],
                rhs=x_codes[:, cols].bitcast(FP8X4),
                rhs_scale=x_plane[:, cols],
                start=True,
                stop=True,
            )
            return bank

        def picked(b, cols):
            return windows[b][:].indirect(offsets[:, cols.start // LIST_ROWS : cols.stop // LIST_ROWS])

        def per_message(name):
            return keep.tile([P, T], F32, name=name, tag=name, align_bytes=64)

        def relu_times(target, bank, gate):
            nc.vector.scalar_tensor_tensor(out=target, in0=bank, scalar=0.0, in1=gate, op0=ALU.max, op1=ALU.mult)

        def sigmoid(target, bank, sign):
            nc.scalar.activation(out=target, in_=bank, func=ACT.Sigmoid, scale=sign)

        whole = slice(0, T)
        halves = [slice(0, T // 2), slice(T // 2, T)]

        load_weights("gate", w2, 0)
        load_scales(0)
        load_scales(1)
        load_weights("cand", w1, 0)
        load_scales(2)
        load_scales(3)
        load_codes()
        load_weights("gate", w2, 1)
        load_weights("cand", w1, 1)
        nc.sync.dma_start(offsets[:], slot)
        load_window(0)
        load_window(1)

        cast("gate", 0, nc.vector.tensor_copy)
        quantise("gate", 0)
        for name, b in (("cand", 0), ("gate", 1), ("cand", 1)):
            cast(name, b, nc.vector.tensor_copy)
            quantise(name, b)

        first, second = halves
        gate0, rest0, gate1, rest1 = (per_message(n) for n in ("gate0", "rest0", "gate1", "rest1"))
        fresh0, fresh1 = per_message("fresh0"), per_message("fresh1")
        old0, kept0, new0, kept1 = (per_message(n) for n in ("old0", "kept0", "new0", "kept1"))

        u0 = [product("gate", 0, cols) for cols in halves]
        v0 = [product("cand", 0, cols) for cols in halves]
        u1 = [product("gate", 1, cols) for cols in halves]
        v1 = [product("cand", 1, cols) for cols in halves]
        for cols, bank in zip(halves, u0):
            sigmoid(gate0[:, cols], bank[:], 1.0)
        sigmoid(rest0[:, first], u0[0][:], -1.0)
        for cols, bank in zip(halves, v0):
            relu_times(fresh0[:, cols], bank[:], gate0[:, cols])

        nc.vector.tensor_tensor(out=kept0[:, first], in0=picked(0, first), in1=rest0[:, first], op=ALU.mult)
        for cols, bank in zip(halves, u1):
            sigmoid(gate1[:, cols], bank[:], 1.0)
        nc.scalar.activation(out=old0[:, second], in_=picked(0, second), func=ACT.Copy)
        for cols, bank in zip(halves, u1):
            sigmoid(rest1[:, cols], bank[:], -1.0)

        nc.vector.tensor_tensor(out=new0[:, first], in0=kept0[:, first], in1=fresh0[:, first], op=ALU.add)
        nc.vector.scalar_tensor_tensor(
            out=kept0[:, second], in0=gate0[:, second], scalar=1.0, in1=old0[:, second], op0=ALU.subtract, op1=ALU.mult
        )
        for cols, bank in zip(halves, v1):
            relu_times(fresh1[:, cols], bank[:], gate1[:, cols])
        nc.vector.tensor_tensor(out=kept1[:], in0=picked(1, whole), in1=rest1[:], op=ALU.mult)
        nc.vector.tensor_tensor(out=new0[:, second], in0=fresh0[:, second], in1=kept0[:, second], op=ALU.subtract)
        for cols in halves:
            nc.scalar.activation(out=picked(0, cols), in_=new0[:, cols], func=ACT.Copy)
        store_window(0)
        nc.vector.tensor_tensor(out=picked(1, whole), in0=kept1[:], in1=fresh1[:], op=ALU.add)
        store_window(1)
